import numpy as np
import ml_dtypes


def mxq(x, axis, fmt="e4m3"):
    dtype, down = {"e4m3": (ml_dtypes.float8_e4m3fn, 7), "e5m2": (ml_dtypes.float8_e5m2, 14)}[fmt]
    v = np.moveaxis(np.asarray(x, np.float32).astype(ml_dtypes.bfloat16).astype(np.float64), axis, -1)
    blocks = v.reshape(v.shape[:-1] + (-1, 32))
    amax = np.abs(blocks).max(-1, keepdims=True)
    byte = np.maximum(np.where(amax > 0, np.frexp(amax)[1] - 1 + 127, 0) - down, 1)
    scale = np.exp2(byte - 127.0)
    codes = (blocks / scale).astype(np.float32).astype(dtype).astype(np.float64)
    return np.moveaxis((codes * scale).reshape(v.shape), -1, axis)


WIDE = False


def mx_kscale(k):
    if not WIDE:
        return np.ones(k)
    levels = np.array([10, -10, 5, -5, 0])
    if k % 512:
        return np.exp2(np.random.permutation(np.resize(levels, k // 32))).repeat(32)
    a = np.empty((k // 512, 16))
    for p in range(k // 512):
        a[p, :8] = np.random.permutation(np.resize(levels, 8))
        for g in range(8):
            far = levels[np.abs(levels - a[p, g]) >= 10]
            a[p, g + 8] = far[np.random.randint(len(far))]
    return np.exp2(a.ravel()).repeat(32)


def f64(x):
    return np.asarray(x).astype(np.float64)


def striped(idx):
    return np.tile(idx.reshape(-1, 16).T, (8, 1)).astype(np.uint16)


def unstriped(offs):
    return offs[:16].T.reshape(-1).astype(np.int64)


E2M1 = np.array([0.0, 0.5, 1.0, 1.5, 2.0, 3.0, 4.0, 6.0, -0.0, -0.5, -1.0, -1.5, -2.0, -3.0, -4.0, -6.0])


def pack_weight(w, fmt):
    k, n = w.shape
    w = f64(np.asarray(w, np.float32).astype(ml_dtypes.bfloat16)).reshape(k // 32, 32, n)
    amax = np.abs(w).max(1)
    if fmt == "e4m3":
        byte = np.frexp(amax)[1] - 1 + 127 - 7
    else:
        mant, ex = np.frexp(amax / 6.0)
        byte = np.where(mant > 0.5, ex, ex - 1) + 127
    byte = np.clip(np.where(amax > 0, byte, 1), 1, 254)
    scaled = (w * np.exp2(127.0 - byte)[:, None, :]).reshape(k, n).astype(np.float32)
    by_word = np.ascontiguousarray(scaled.reshape(k // 512, 128, 4, n).transpose(0, 1, 3, 2))
    if fmt == "e4m3":
        words = by_word.astype(ml_dtypes.float8_e4m3fn).view(np.uint8)
    else:
        c = by_word.astype(ml_dtypes.float4_e2m1fn).view(np.uint8) & 0xF
        words = (c[..., 0::2] | (c[..., 1::2] << 4)).reshape(k // 512, 128, 2 * n)
    return np.ascontiguousarray(words), np.ascontiguousarray(byte.astype(np.uint8).reshape(k // 512, 16, n))


def unpack_weight(words, scales, fmt):
    g, _, n = scales.shape
    words = np.ascontiguousarray(words).reshape(g, 128, n, -1)
    if fmt == "e4m3":
        vals = words.view(ml_dtypes.float8_e4m3fn).astype(np.float64)
    else:
        nib = np.empty((g, 128, n, 4), np.uint8)
        nib[..., 0::2] = words & 0xF
        nib[..., 1::2] = words >> 4
        vals = E2M1[nib]
    vals = vals * np.repeat(np.exp2(scales.astype(np.float64) - 127.0), 8, axis=1)[..., None]
    return vals.transpose(0, 1, 3, 2).reshape(g * 512, n)


def relu2(v):
    return np.maximum(v, 0.0) ** 2


K, T, E, C, H, N = 2048, 512, 4, 256, 512, 384


def by_expert(wq, xq):
    return np.concatenate([wq[e].T @ xq[:, e * C:(e + 1) * C] for e in range(E)], axis=1)


def setup_inputs():
    n = np.random.standard_normal
    s = mx_kscale(K)[:, None]
    u = mx_kscale(H)
    first = np.random.permutation(np.repeat(np.arange(E), T // E))
    second = (first + 1 + np.random.permutation(np.repeat(np.arange(E - 1), -(-T // (E - 1)))[:T])) % E
    while np.bincount(second, minlength=E).max() != T // E:
        load = np.bincount(second, minlength=E); hi, lo = int(load.argmax()), int(load.argmin())
        t = np.flatnonzero((second == hi) & (first != lo))[0]; second[t] = lo
    slot_token = np.empty(E * C, np.int64); pos = np.empty((2, T), np.int64); fill = np.zeros(E, np.int64)
    place = np.stack([np.random.permutation(C) for _ in range(E)])
    for r, deal in enumerate((first, second)):
        for t in np.random.permutation(T):
            e = deal[t]; j = e * C + place[e, fill[e]]; fill[e] += 1; slot_token[j] = t; pos[r, t] = j
    g = np.random.uniform(0.2, 0.8, T)
    w1 = [pack_weight(m, "e2m1") for m in n((E, K, H)) / np.sqrt(K) / s[None] * u[None, None, :]]
    w2 = [pack_weight(m, "e2m1") for m in n((E, H, N)) / np.sqrt(H) / u[None, :, None] ** 2]
    return {
        "xT": (n((K, T)) * s).astype(np.float32),
        "w1_words": np.stack([m[0] for m in w1]),
        "w1_scales": np.stack([m[1] for m in w1]),
        "w2_words": np.stack([m[0] for m in w2]),
        "w2_scales": np.stack([m[1] for m in w2]),
        "gate": np.stack([np.tile(g, (N, 1)), np.tile(1.0 - g, (N, 1))]).astype(np.float32),
        "offs": striped(slot_token),
        "pos1": striped(pos[0]),
        "pos2": striped(pos[1]),
    }


def reference(xT, w1_words, w1_scales, w2_words, w2_scales, gate, offs, pos1, pos2):
    idx = unstriped(offs)
    w1 = np.stack([unpack_weight(w1_words[e], w1_scales[e], "e2m1") for e in range(E)])
    w2 = np.stack([unpack_weight(w2_words[e], w2_scales[e], "e2m1") for e in range(E)])
    xq = mxq(f64(xT)[:, idx], 0, "e4m3")
    h = relu2(by_expert(w1, xq))
    y = by_expert(w2, mxq(h, 0, "e4m3"))
    return f64(gate[0]) * y[:, unstriped(pos1)] + f64(gate[1]) * y[:, unstriped(pos2)]

@@ -1,0 +1,271 @@
+from contextlib import ExitStack
+
+import concourse.mybir as mybir
+from concourse.masks import make_identity
+
+K, T, E, C, H, N = 2048, 512, 4, 256, 512, 384
+P = 128
+PASSES = K // 512
+SLOTS = E * C
+FLOPS = 2 * SLOTS * (K * H + H * N)
+
+F32 = mybir.dt.float32
+BF16 = mybir.dt.bfloat16
+I32 = mybir.dt.int32
+U32 = mybir.dt.uint32
+U16 = mybir.dt.uint16
+U8 = mybir.dt.uint8
+FP8X4 = mybir.dt.float8_e4m3fn_x4
+FP4X4 = mybir.dt.float4_e2m1fn_x4
+RELU = mybir.ActivationFunctionType.Relu
+SQUARE = mybir.ActivationFunctionType.Square
+MULT = mybir.AluOpType.mult
+ADD = mybir.AluOpType.add
+
+VECTOR_TOKENS = (256, 64, 0, 128)
+VECTOR_RELU = (5, 7)
+VECTOR_Y = ((2, 1), (3, 0))
+
+
+def tile_moe_pln_mlp_relu2_kernel(
+    tc, xT, w1_words, w1_scales, w2_words, w2_scales, gate, offs, pos1, pos2, out
+):
+    nc = tc.nc
+    with ExitStack() as ctx:
+        lists = ctx.enter_context(tc.tile_pool(name="lists", bufs=1))
+        keep = ctx.enter_context(tc.tile_pool(name="keep", bufs=1))
+        work = ctx.enter_context(tc.tile_pool(name="work", bufs=4))
+        stage = ctx.enter_context(tc.tile_pool(name="stage", bufs=4))
+        psum = ctx.enter_context(tc.psum_pool(name="psum", bufs=5))
+        aux = ctx.enter_context(tc.psum_pool(name="aux", bufs=3))
+        late = ctx.enter_context(tc.tile_pool(name="late", bufs=1))
+
+        offs_t = lists.tile([P, SLOTS // 16], U16, name="offs_t")
+        pos1_t = lists.tile([P, T // 16], U16, name="pos1_t")
+        pos2_t = lists.tile([P, T // 16], U16, name="pos2_t")
+
+        raw = [stage.tile([P, 4, T], F32, name="raw%d" % s, tag="raw", align_bytes=64) for s in range(PASSES)]
+        xb = [keep.tile([P, T, 4], BF16, name="xb%d" % s, align_bytes=64) for s in range(PASSES)]
+        xw = keep.tile([P, PASSES * T], U32, name="xw", align_bytes=64)
+        xs = late.tile([P, 2 * T], U8, name="xs", tag="late", align_bytes=64)
+        gw = {}
+        gs = {}
+        gp = [keep.tile([P, SLOTS], U8, name="gp%d" % h, align_bytes=64) for h in range(2)]
+        w1w = [keep.tile([P, PASSES * 2 * H], U8, name="w1w%d" % e, align_bytes=64) for e in range(2)]
+        w1s = keep.tile([P, E * PASSES * H], U8, name="w1s", align_bytes=64)
+        w2w = stage.tile([P, E * 2 * N], U8, name="w2w", tag="raw", align_bytes=64)
+        w1w += [stage.tile([P, PASSES * 2 * H], U8, name="w1w%d" % e, tag="raw", align_bytes=64) for e in (2, 3)]
+        w2s = keep.tile([P, E * N], U8, name="w2s", align_bytes=64)
+        hw = keep.tile([P, SLOTS], U32, name="hw", align_bytes=64)
+        hs = keep.tile([P, SLOTS], U8, name="hs", align_bytes=64)
+        y = [keep.tile([P, SLOTS], F32, name="y%d" % j) for j in range(N // P)]
+        ident = keep.tile([P, P], F32, name="ident")
+
+        xT_v = xT.rearrange("(s p j) t -> s p j t", p=P, j=4)
+        w1w_v = w1_words.bitcast(I32)
+        w1s_v = w1_scales.bitcast(I32)
+        w2w_v = w2_words.bitcast(I32)
+        w2s_v = w2_scales.bitcast(I32)
+
+        nc.sync.dma_start(offs_t[:], offs)
+        half = T // 2
+        nc.sync.dma_start(out=raw[0][:, :, 0:half], in_=xT_v[0][:, :, 0:half])
+        nc.sync.dma_start(out=raw[0][:, :, half:T], in_=xT_v[0][:, :, half:T])
+        for s in range(1, PASSES):
+            nc.sync.dma_start(out=raw[s][:], in_=xT_v[s])
+
+        nc.vector.memset(w1s[:].bitcast(I32), 0)
+        nc.vector.memset(w2s[:].bitcast(I32), 0)
+        nc.gpsimd.memset(xs[:], 0)
+        for h in range(2):
+            nc.gpsimd.memset(gp[h][:], 0)
+        make_identity(nc, ident[:])
+
+        def load_w1(e):
+            nc.sync.dma_start(
+                out=w1w[e][:].bitcast(I32).rearrange("p (s b) -> p s b", s=PASSES),
+                in_=w1w_v[e].rearrange("s p b -> p s b"),
+            )
+
+        for q in range(4):
+            nc.sync.dma_start(
+                out=w1s[32 * q : 32 * q + 4, :].bitcast(I32).rearrange("p (a b) -> p a b", b=H // 4),
+                in_=w1s_v[:, :, 4 * q : 4 * q + 4, :].rearrange("e s r b -> r (e s) b"),
+            )
+        load_w1(0)
+        load_w1(1)
+
+        def cast(s, lo, hi, engine):
+            if hi <= lo:
+                return
+            dst = xb[s][:, lo:hi, :].rearrange("p (c i) t -> p c t i", i=4)
+            src = raw[s][:, :, lo:hi].rearrange("p t (c i) -> p c t i", i=4)
+            if engine == "vector":
+                nc.vector.tensor_copy(dst, src)
+            else:
+                nc.scalar.copy(dst, src)
+
+        def quantise(s, lo, hi):
+            row = 4 * (s % 2)
+            nc.vector.quantize_mx(
+                out=xw[:, s * T + lo : s * T + hi].bitcast(FP8X4),
+                scales=xs[row:P, s // 2 * T + lo : s // 2 * T + hi],
+                in_=xb[s][:, lo:hi, :].rearrange("p c t -> p (c t)"),
+            )
+
+        def words(s, e, wide=False, pool=keep, tag=None, bufs=1):
+            tag = tag or "gw%d%d" % (s, e)
+            gw[s, e] = pool.tile([P, C], U32, name="gw%d%d" % (s, e), tag=tag, bufs=bufs, align_bytes=64)
+            end = PASSES * T if wide else (s + 1) * T
+            nc.vector.tensor_copy(
+                gw[s, e][:], xw[:, s * T : end].indirect(offs_t[:, e * C // 16 : (e + 1) * C // 16])
+            )
+
+        def scales(h, e, wide=False, pool=keep, tag=None, bufs=1):
+            tag = tag or "gs%d%d" % (h, e)
+            gs[h, e] = pool.tile([P, C], U8, name="gs%d%d" % (h, e), tag=tag, bufs=bufs, align_bytes=64)
+            end = 2 * T if wide else (h + 1) * T
+            nc.vector.tensor_copy(
+                gs[h, e][:], xs[:, h * T : end].indirect(offs_t[:, e * C // 16 : (e + 1) * C // 16])
+            )
+            nc.sync.dma_start(
+                out=gp[h][0 : P - 4, e * C : (e + 1) * C].bitcast(I32),
+                in_=gs[h, e][4:P, :].bitcast(I32),
+            )
+
+        acc = {}
+
+        def first(s, b):
+            e = b // 2
+            if s == 0:
+                acc[b] = psum.tile([P, H], F32, name="bank")
+            cols = slice(b % 2 * P, (b % 2 + 1) * P)
+            plane = gs[s // 2, e][:, cols] if s % 2 == 0 else gp[s // 2][:, b * P : (b + 1) * P]
+            w = (e * PASSES + s) * H
+            nc.tensor.matmul_mx(
+                out=acc[b][:],
+                lhsT=gw[s, e][:, cols].bitcast(FP8X4),
+                lhsT_scale=plane,
+                rhs=w1w[e][:, s * 2 * H : (s + 1) * 2 * H].bitcast(FP4X4),
+                rhs_scale=w1s[:, w : w + H],
+                start=(s == 0),
+                stop=(s == PASSES - 1),
+            )
+
+        def hidden(b):
+            cols = slice(b * P, (b + 1) * P)
+            r = work.tile([P, 4, P], F32, name="r", tag="r%d" % b if b < 2 else "r", align_bytes=64, bufs=1 if b < 2 else 3)
+            lanes = acc[b][:].rearrange("p (m t) -> p t m", t=4)
+            if b in VECTOR_RELU:
+                nc.vector.tensor_scalar_max(r[:], lanes, 0.0)
+            else:
+                nc.scalar.activation(r[:], lanes, RELU)
+            turned = aux.tile([P, 4, P], F32, name="aux")
+            for t in range(4):
+                nc.tensor.transpose(turned[:, t, :], r[:, t, :], ident[:])
+            hb = work.tile([P, P, 4], BF16, name="hb", tag="hb%d" % b if b < 3 else "hb", align_bytes=64, bufs=1 if b < 3 else 3)
+            nc.scalar.activation(hb[:], turned[:].rearrange("p t n -> p n t"), SQUARE)
+            nc.vector.quantize_mx(
+                out=hw[:, cols].bitcast(FP8X4),
+                scales=hs[:, cols],
+                in_=hb[:].rearrange("p n t -> p (n t)"),
+            )
+
+        def second(e, lo, hi):
+            for j in range(N // P):
+                bank = aux.tile([P, H], F32, name="aux")
+                w = e * N + j * P
+                nc.tensor.matmul_mx(
+                    out=bank[:, 0 : hi - lo],
+                    lhsT=w2w[:, 2 * w : 2 * (w + P)].bitcast(FP4X4),
+                    lhsT_scale=w2s[:, w : w + P],
+                    rhs=hw[:, lo:hi].bitcast(FP8X4),
+                    rhs_scale=hs[:, lo:hi],
+                    start=True,
+                    stop=True,
+                )
+                if (e, j) in VECTOR_Y:
+                    nc.vector.tensor_copy(y[j][:, lo:hi], bank[:, 0 : hi - lo])
+                else:
+                    nc.scalar.copy(y[j][:, lo:hi], bank[:, 0 : hi - lo])
+
+        def load_tokens(s):
+            v = VECTOR_TOKENS[s]
+            cast(s, 0, v, "vector")
+            cast(s, v, T, "scalar")
+            if s == 0:
+                quantise(s, 0, half)
+                quantise(s, half, T)
+            else:
+                quantise(s, 0, T)
+
+        def products(s, e):
+            first(s, 2 * e)
+            first(s, 2 * e + 1)
+
+        load_tokens(0)
+        for e in range(E):
+            words(0, e)
+        load_tokens(1)
+        for e in (0, 1):
+            scales(0, e)
+        for e in (0, 1):
+            words(1, e)
+            products(0, e)
+            products(1, e)
+        load_w1(2)
+        load_w1(3)
+        for q in range(4):
+            nc.sync.dma_start(
+                out=w2s[32 * q : 32 * q + 4, :].bitcast(I32).rearrange("p (a b) -> p a b", b=N // 4),
+                in_=w2s_v[:, 0, 4 * q : 4 * q + 4, :].rearrange("e r b -> r e b"),
+            )
+        nc.sync.dma_start(
+            out=w2w[:].bitcast(I32).rearrange("p (e b) -> p e b", e=E),
+            in_=w2w_v[:, 0].rearrange("e p b -> p e b"),
+        )
+        nc.sync.dma_start(pos1_t[:], pos1)
+        nc.sync.dma_start(pos2_t[:], pos2)
+        load_tokens(2)
+        load_tokens(3)
+        for e in (0, 1):
+            scales(1, e)
+            words(2, e, wide=True)
+            words(3, e)
+            products(2, e)
+        scales(0, 2, wide=True)
+        scales(1, 2)
+        for s in range(1, PASSES):
+            words(s, 2, wide=True)
+        for b in range(2):
+            first(3, b)
+            hidden(b)
+        second(0, 0, C)
+        scales(0, 3, wide=True, pool=work, bufs=1, tag="r0")
+        scales(1, 3, pool=work, bufs=1, tag="r1")
+        first(3, 2)
+        hidden(2)
+        words(1, 3, wide=True, pool=work, bufs=1, tag="hb0")
+        words(2, 3, wide=True, pool=work, bufs=1, tag="hb1")
+        words(3, 3, pool=work, bufs=1, tag="hb2")
+        g = late.tile([P, N // P, 2, T], F32, name="g", tag="late", align_bytes=64)
+        for j in range(N // P):
+            nc.sync.dma_start(out=g[:, j], in_=gate[:, j * P : (j + 1) * P, :].rearrange("g p t -> p g t"))
+        first(3, 3)
+        hidden(3)
+        second(1, C, 2 * C)
+        for e in (2, 3):
+            for b in (2 * e, 2 * e + 1):
+                for s in range(PASSES):
+                    first(s, b)
+                hidden(b)
+            second(e, e * C, (e + 1) * C)
+
+        for j in range(N // P):
+            a = work.tile([P, T], F32, name="a")
+            b = work.tile([P, T], F32, name="b")
+            o = work.tile([P, T], F32, name="o")
+            nc.vector.tensor_tensor(a[:], y[j][:].indirect(pos1_t[:]), g[:, j, 0, :], MULT)
+            nc.vector.tensor_tensor(b[:], y[j][:].indirect(pos2_t[:]), g[:, j, 1, :], MULT)
+            nc.vector.tensor_tensor(o[:], a[:], b[:], ADD)
+            nc.sync.dma_start(out=out[j * P : (j + 1) * P, :], in_=o[:])

@@ -23,8 +23,7 @@ MULT = mybir.AluOpType.mult
 ADD = mybir.AluOpType.add
 
 VECTOR_TOKENS = (256, 64, 0, 128)
-VECTOR_RELU = (5, 7)
-VECTOR_Y = ((2, 1), (3, 0))
+VECTOR_RELU = (6, 7)
 
 
 def tile_moe_pln_mlp_relu2_kernel(
@@ -49,7 +48,7 @@ def tile_moe_pln_mlp_relu2_kernel(
         xw = keep.tile([P, PASSES * T], U32, name="xw", align_bytes=64)
         xs = late.tile([P, 2 * T], U8, name="xs", tag="late", align_bytes=64)
         gw = {}
-        gs = {}
+        gs = [keep.tile([P, SLOTS], U8, name="gs%d" % h, align_bytes=64) for h in range(2)]
         gp = [keep.tile([P, SLOTS], U8, name="gp%d" % h, align_bytes=64) for h in range(2)]
         w1w = [keep.tile([P, PASSES * 2 * H], U8, name="w1w%d" % e, align_bytes=64) for e in range(2)]
         w1s = keep.tile([P, E * PASSES * H], U8, name="w1s", align_bytes=64)
@@ -67,33 +66,32 @@ def tile_moe_pln_mlp_relu2_kernel(
         w2w_v = w2_words.bitcast(I32)
         w2s_v = w2_scales.bitcast(I32)
 
-        nc.sync.dma_start(offs_t[:], offs)
-        half = T // 2
-        nc.sync.dma_start(out=raw[0][:, :, 0:half], in_=xT_v[0][:, :, 0:half])
-        nc.sync.dma_start(out=raw[0][:, :, half:T], in_=xT_v[0][:, :, half:T])
-        for s in range(1, PASSES):
-            nc.sync.dma_start(out=raw[s][:], in_=xT_v[s])
-
-        nc.vector.memset(w1s[:].bitcast(I32), 0)
-        nc.vector.memset(w2s[:].bitcast(I32), 0)
-        nc.gpsimd.memset(xs[:], 0)
-        for h in range(2):
-            nc.gpsimd.memset(gp[h][:], 0)
-        make_identity(nc, ident[:])
-
         def load_w1(e):
             nc.sync.dma_start(
                 out=w1w[e][:].bitcast(I32).rearrange("p (s b) -> p s b", s=PASSES),
                 in_=w1w_v[e].rearrange("s p b -> p s b"),
             )
 
+        half = T // 2
+        nc.sync.dma_start(offs_t[:], offs)
+        nc.sync.dma_start(out=raw[0][:, :, 0:half], in_=xT_v[0][:, :, 0:half])
+        nc.sync.dma_start(out=raw[0][:, :, half:T], in_=xT_v[0][:, :, half:T])
+        nc.sync.dma_start(out=raw[1][:], in_=xT_v[1])
+        nc.vector.memset(w1s[:].bitcast(I32), 0)
         for q in range(4):
             nc.sync.dma_start(
                 out=w1s[32 * q : 32 * q + 4, :].bitcast(I32).rearrange("p (a b) -> p a b", b=H // 4),
                 in_=w1s_v[:, :, 4 * q : 4 * q + 4, :].rearrange("e s r b -> r (e s) b"),
             )
+        nc.sync.dma_start(out=raw[2][:], in_=xT_v[2])
         load_w1(0)
+        nc.sync.dma_start(out=raw[3][:], in_=xT_v[3])
         load_w1(1)
+        nc.gpsimd.memset(xs[:], 0)
+        for h in range(2):
+            nc.gpsimd.memset(gp[h][:], 0)
+        nc.vector.memset(w2s[:].bitcast(I32), 0)
+        make_identity(nc, ident[:])
 
         def cast(s, lo, hi, engine):
             if hi <= lo:
@@ -113,25 +111,26 @@ def tile_moe_pln_mlp_relu2_kernel(
                 in_=xb[s][:, lo:hi, :].rearrange("p c t -> p (c t)"),
             )
 
-        def words(s, e, wide=False, pool=keep, tag=None, bufs=1):
-            tag = tag or "gw%d%d" % (s, e)
-            gw[s, e] = pool.tile([P, C], U32, name="gw%d%d" % (s, e), tag=tag, bufs=bufs, align_bytes=64)
+        def words(s, e, wide=False):
             end = PASSES * T if wide else (s + 1) * T
+            gw[s, e] = keep.tile([P, C], U32, name="gw%d%d" % (s, e), align_bytes=64)
             nc.vector.tensor_copy(
                 gw[s, e][:], xw[:, s * T : end].indirect(offs_t[:, e * C // 16 : (e + 1) * C // 16])
             )
 
-        def scales(h, e, wide=False, pool=keep, tag=None, bufs=1):
-            tag = tag or "gs%d%d" % (h, e)
-            gs[h, e] = pool.tile([P, C], U8, name="gs%d%d" % (h, e), tag=tag, bufs=bufs, align_bytes=64)
+        def scales(h, experts, wide=False):
             end = 2 * T if wide else (h + 1) * T
-            nc.vector.tensor_copy(
-                gs[h, e][:], xs[:, h * T : end].indirect(offs_t[:, e * C // 16 : (e + 1) * C // 16])
-            )
-            nc.sync.dma_start(
-                out=gp[h][0 : P - 4, e * C : (e + 1) * C].bitcast(I32),
-                in_=gs[h, e][4:P, :].bitcast(I32),
-            )
+            for e in experts:
+                nc.vector.tensor_copy(
+                    gs[h][:, e * C : (e + 1) * C],
+                    xs[:, h * T : end].indirect(offs_t[:, e * C // 16 : (e + 1) * C // 16]),
+                )
+            cols = slice(experts[0] * C, (experts[-1] + 1) * C)
+            for q in range(4):
+                nc.sync.dma_start(
+                    out=gp[h][32 * q : 32 * q + 4, cols].bitcast(I32),
+                    in_=gs[h][32 * q + 4 : 32 * q + 8, cols].bitcast(I32),
+                )
 
         acc = {}
 
@@ -140,7 +139,7 @@ def tile_moe_pln_mlp_relu2_kernel(
             if s == 0:
                 acc[b] = psum.tile([P, H], F32, name="bank")
             cols = slice(b % 2 * P, (b % 2 + 1) * P)
-            plane = gs[s // 2, e][:, cols] if s % 2 == 0 else gp[s // 2][:, b * P : (b + 1) * P]
+            plane = (gs if s % 2 == 0 else gp)[s // 2][:, b * P : (b + 1) * P]
             w = (e * PASSES + s) * H
             nc.tensor.matmul_mx(
                 out=acc[b][:],
@@ -154,7 +153,7 @@ def tile_moe_pln_mlp_relu2_kernel(
 
         def hidden(b):
             cols = slice(b * P, (b + 1) * P)
-            r = work.tile([P, 4, P], F32, name="r", tag="r%d" % b if b < 2 else "r", align_bytes=64, bufs=1 if b < 2 else 3)
+            r = work.tile([P, 4, P], F32, name="r", align_bytes=64)
             lanes = acc[b][:].rearrange("p (m t) -> p t m", t=4)
             if b in VECTOR_RELU:
                 nc.vector.tensor_scalar_max(r[:], lanes, 0.0)
@@ -163,7 +162,7 @@ def tile_moe_pln_mlp_relu2_kernel(
             turned = aux.tile([P, 4, P], F32, name="aux")
             for t in range(4):
                 nc.tensor.transpose(turned[:, t, :], r[:, t, :], ident[:])
-            hb = work.tile([P, P, 4], BF16, name="hb", tag="hb%d" % b if b < 3 else "hb", align_bytes=64, bufs=1 if b < 3 else 3)
+            hb = keep.tile([P, P, 4], BF16, name="hb%d" % b, align_bytes=64)
             nc.scalar.activation(hb[:], turned[:].rearrange("p t n -> p n t"), SQUARE)
             nc.vector.quantize_mx(
                 out=hw[:, cols].bitcast(FP8X4),
@@ -171,23 +170,23 @@ def tile_moe_pln_mlp_relu2_kernel(
                 in_=hb[:].rearrange("p n t -> p (n t)"),
             )
 
-        def second(e, lo, hi):
-            for j in range(N // P):
-                bank = aux.tile([P, H], F32, name="aux")
-                w = e * N + j * P
-                nc.tensor.matmul_mx(
-                    out=bank[:, 0 : hi - lo],
-                    lhsT=w2w[:, 2 * w : 2 * (w + P)].bitcast(FP4X4),
-                    lhsT_scale=w2s[:, w : w + P],
-                    rhs=hw[:, lo:hi].bitcast(FP8X4),
-                    rhs_scale=hs[:, lo:hi],
-                    start=True,
-                    stop=True,
-                )
-                if (e, j) in VECTOR_Y:
-                    nc.vector.tensor_copy(y[j][:, lo:hi], bank[:, 0 : hi - lo])
-                else:
-                    nc.scalar.copy(y[j][:, lo:hi], bank[:, 0 : hi - lo])
+        def second(e, j, bank):
+            w = e * N + j * P
+            nc.tensor.matmul_mx(
+                out=bank,
+                lhsT=w2w[:, 2 * w : 2 * (w + P)].bitcast(FP4X4),
+                lhsT_scale=w2s[:, w : w + P],
+                rhs=hw[:, e * C : (e + 1) * C].bitcast(FP8X4),
+                rhs_scale=hs[:, e * C : (e + 1) * C],
+                start=True,
+                stop=True,
+            )
+
+        def move(dst, src, engine):
+            if engine == "v":
+                nc.vector.tensor_copy(dst, src)
+            else:
+                nc.scalar.copy(dst, src)
 
         def load_tokens(s):
             v = VECTOR_TOKENS[s]
@@ -199,20 +198,16 @@ def tile_moe_pln_mlp_relu2_kernel(
             else:
                 quantise(s, 0, T)
 
-        def products(s, e):
-            first(s, 2 * e)
-            first(s, 2 * e + 1)
-
         load_tokens(0)
         for e in range(E):
             words(0, e)
         load_tokens(1)
-        for e in (0, 1):
-            scales(0, e)
+        scales(0, (0, 1))
         for e in (0, 1):
             words(1, e)
-            products(0, e)
-            products(1, e)
+            for b in (2 * e, 2 * e + 1):
+                first(0, b)
+                first(1, b)
         load_w1(2)
         load_w1(3)
         for q in range(4):
@@ -229,37 +224,36 @@ def tile_moe_pln_mlp_relu2_kernel(
         load_tokens(2)
         load_tokens(3)
         for e in (0, 1):
-            scales(1, e)
+            scales(1, (e,))
             words(2, e, wide=True)
             words(3, e)
-            products(2, e)
-        scales(0, 2, wide=True)
-        scales(1, 2)
-        for s in range(1, PASSES):
-            words(s, 2, wide=True)
-        for b in range(2):
-            first(3, b)
-            hidden(b)
-        second(0, 0, C)
-        scales(0, 3, wide=True, pool=work, bufs=1, tag="r0")
-        scales(1, 3, pool=work, bufs=1, tag="r1")
-        first(3, 2)
-        hidden(2)
-        words(1, 3, wide=True, pool=work, bufs=1, tag="hb0")
-        words(2, 3, wide=True, pool=work, bufs=1, tag="hb1")
-        words(3, 3, pool=work, bufs=1, tag="hb2")
+            for b in (2 * e, 2 * e + 1):
+                first(2, b)
+        scales(0, (2, 3), wide=True)
+        scales(1, (2, 3))
+        for e in (2, 3):
+            for s in range(1, PASSES):
+                words(s, e, wide=True)
         g = late.tile([P, N // P, 2, T], F32, name="g", tag="late", align_bytes=64)
         for j in range(N // P):
             nc.sync.dma_start(out=g[:, j], in_=gate[:, j * P : (j + 1) * P, :].rearrange("g p t -> p g t"))
-        first(3, 3)
-        hidden(3)
-        second(1, C, 2 * C)
+        for b in range(4):
+            first(3, b)
+            hidden(b)
+        for b in range(4, 8):
+            for s in range(PASSES):
+                first(s, b)
+            hidden(b)
+        for j in range(N // P):
+            bank = aux.tile([P, H], F32, name="aux")
+            second(0, j, bank[:, 0:C])
+            second(1, j, bank[:, C : 2 * C])
+            move(y[j][:, 0 : 2 * C], bank[:], "vvv"[j])
         for e in (2, 3):
-            for b in (2 * e, 2 * e + 1):
-                for s in range(PASSES):
-                    first(s, b)
-                hidden(b)
-            second(e, e * C, (e + 1) * C)
+            for j in range(N // P):
+                bank = aux.tile([P, H], F32, name="aux")
+                second(e, j, bank[:, 0:C])
+                move(y[j][:, e * C : (e + 1) * C], bank[:, 0:C], ("svs", "vss")[e - 2][j])
 
         for j in range(N // P):
             a = work.tile([P, T], F32, name="a")

@@ -22,9 +22,6 @@ SQUARE = mybir.ActivationFunctionType.Square
 MULT = mybir.AluOpType.mult
 ADD = mybir.AluOpType.add
 
-VECTOR_TOKENS = (256, 64, 0, 128)
-VECTOR_RELU = (6, 7)
-
 
 def tile_moe_pln_mlp_relu2_kernel(
     tc, xT, w1_words, w1_scales, w2_words, w2_scales, gate, offs, pos1, pos2, out
@@ -34,31 +31,15 @@ def tile_moe_pln_mlp_relu2_kernel(
         lists = ctx.enter_context(tc.tile_pool(name="lists", bufs=1))
         keep = ctx.enter_context(tc.tile_pool(name="keep", bufs=1))
         work = ctx.enter_context(tc.tile_pool(name="work", bufs=4))
-        stage = ctx.enter_context(tc.tile_pool(name="stage", bufs=4))
         psum = ctx.enter_context(tc.psum_pool(name="psum", bufs=5))
         aux = ctx.enter_context(tc.psum_pool(name="aux", bufs=3))
-        late = ctx.enter_context(tc.tile_pool(name="late", bufs=1))
+
+        def hold(shape, dtype, name, tag=None):
+            return keep.tile(shape, dtype, name=name, tag=tag or name, align_bytes=64)
 
         offs_t = lists.tile([P, SLOTS // 16], U16, name="offs_t")
         pos1_t = lists.tile([P, T // 16], U16, name="pos1_t")
         pos2_t = lists.tile([P, T // 16], U16, name="pos2_t")
-
-        raw = [stage.tile([P, 4, T], F32, name="raw%d" % s, tag="raw", align_bytes=64) for s in range(PASSES)]
-        xb = [keep.tile([P, T, 4], BF16, name="xb%d" % s, align_bytes=64) for s in range(PASSES)]
-        xw = keep.tile([P, PASSES * T], U32, name="xw", align_bytes=64)
-        xs = late.tile([P, 2 * T], U8, name="xs", tag="late", align_bytes=64)
-        gw = {}
-        gs = [keep.tile([P, SLOTS], U8, name="gs%d" % h, align_bytes=64) for h in range(2)]
-        gp = [keep.tile([P, SLOTS], U8, name="gp%d" % h, align_bytes=64) for h in range(2)]
-        w1w = [keep.tile([P, PASSES * 2 * H], U8, name="w1w%d" % e, align_bytes=64) for e in range(2)]
-        w1s = keep.tile([P, E * PASSES * H], U8, name="w1s", align_bytes=64)
-        w2w = stage.tile([P, E * 2 * N], U8, name="w2w", tag="raw", align_bytes=64)
-        w1w += [stage.tile([P, PASSES * 2 * H], U8, name="w1w%d" % e, tag="raw", align_bytes=64) for e in (2, 3)]
-        w2s = keep.tile([P, E * N], U8, name="w2s", align_bytes=64)
-        hw = keep.tile([P, SLOTS], U32, name="hw", align_bytes=64)
-        hs = keep.tile([P, SLOTS], U8, name="hs", align_bytes=64)
-        y = [keep.tile([P, SLOTS], F32, name="y%d" % j) for j in range(N // P)]
-        ident = keep.tile([P, P], F32, name="ident")
 
         xT_v = xT.rearrange("(s p j) t -> s p j t", p=P, j=4)
         w1w_v = w1_words.bitcast(I32)
@@ -66,71 +47,98 @@ def tile_moe_pln_mlp_relu2_kernel(
         w2w_v = w2_words.bitcast(I32)
         w2s_v = w2_scales.bitcast(I32)
 
-        def load_w1(e):
+        half = T // 2
+        raw = {}
+        for i in range(2):
+            raw[0, i] = hold([P, 4, half], F32, "raw0%d" % i)
+        for s in range(1, PASSES):
+            raw[s, 0] = hold([P, 4, T], F32, "raw%d" % s)
+        xb = [hold([P, T, 4], BF16, "xb%d" % s) for s in range(PASSES)]
+        xw = hold([P, PASSES * T], U32, "xw")
+        xs = hold([P, 2 * T], U8, "xs")
+        gw = {}
+        gs = [hold([P, SLOTS], U8, "gs%d" % h) for h in range(2)]
+        gp = [hold([P, SLOTS], U8, "gp%d" % h) for h in range(2)]
+        w1s = hold([P, E * PASSES * H], U8, "w1s")
+        w1w = {}
+        hw = hold([P, SLOTS], U32, "hw")
+        hs = hold([P, SLOTS], U8, "hs")
+        y = [hold([P, SLOTS], F32, "y%d" % j) for j in range(N // P)]
+        ident = hold([P, P], F32, "ident")
+
+        def load_x(s, i=0):
+            lo = i * half
+            n = half if s == 0 else T
+            nc.sync.dma_start(out=raw[s, i][:], in_=xT_v[s][:, :, lo : lo + n])
+
+        def load_w1(e, tag=None):
+            w1w[e] = hold([P, PASSES * 2 * H], U8, "w1w%d" % e, tag)
             nc.sync.dma_start(
                 out=w1w[e][:].bitcast(I32).rearrange("p (s b) -> p s b", s=PASSES),
                 in_=w1w_v[e].rearrange("s p b -> p s b"),
             )
 
-        half = T // 2
+        def load_w1_scales():
+            for q in range(4):
+                nc.gpsimd.dma_start(
+                    out=w1s[32 * q : 32 * q + 4, :].bitcast(I32).rearrange("p (a b) -> p a b", b=H // 4),
+                    in_=w1s_v[:, :, 4 * q : 4 * q + 4, :].rearrange("e s r b -> r (e s) b"),
+                )
+
         nc.sync.dma_start(offs_t[:], offs)
-        nc.sync.dma_start(out=raw[0][:, :, 0:half], in_=xT_v[0][:, :, 0:half])
-        nc.sync.dma_start(out=raw[0][:, :, half:T], in_=xT_v[0][:, :, half:T])
-        nc.sync.dma_start(out=raw[1][:], in_=xT_v[1])
         nc.vector.memset(w1s[:].bitcast(I32), 0)
-        for q in range(4):
-            nc.sync.dma_start(
-                out=w1s[32 * q : 32 * q + 4, :].bitcast(I32).rearrange("p (a b) -> p a b", b=H // 4),
-                in_=w1s_v[:, :, 4 * q : 4 * q + 4, :].rearrange("e s r b -> r (e s) b"),
-            )
-        nc.sync.dma_start(out=raw[2][:], in_=xT_v[2])
-        load_w1(0)
-        nc.sync.dma_start(out=raw[3][:], in_=xT_v[3])
-        load_w1(1)
+
         nc.gpsimd.memset(xs[:], 0)
         for h in range(2):
-            nc.gpsimd.memset(gp[h][:], 0)
-        nc.vector.memset(w2s[:].bitcast(I32), 0)
+            nc.gpsimd.memset(gp[h][:].bitcast(I32), 0)
         make_identity(nc, ident[:])
 
+
         def cast(s, lo, hi, engine):
-            if hi <= lo:
-                return
-            dst = xb[s][:, lo:hi, :].rearrange("p (c i) t -> p c t i", i=4)
-            src = raw[s][:, :, lo:hi].rearrange("p t (c i) -> p c t i", i=4)
-            if engine == "vector":
-                nc.vector.tensor_copy(dst, src)
-            else:
-                nc.scalar.copy(dst, src)
+            if hi > lo:
+                i, base = (lo // half, lo // half * half) if s == 0 else (0, 0)
+                dst = xb[s][:, lo:hi, :].rearrange("p (c i) t -> p c t i", i=4)
+                src = raw[s, i][:, :, lo - base : hi - base].rearrange("p t (c i) -> p c t i", i=4)
+                if engine == "v":
+                    nc.vector.tensor_copy(dst, src)
+                else:
+                    nc.scalar.copy(dst, src)
 
         def quantise(s, lo, hi):
-            row = 4 * (s % 2)
             nc.vector.quantize_mx(
                 out=xw[:, s * T + lo : s * T + hi].bitcast(FP8X4),
-                scales=xs[row:P, s // 2 * T + lo : s // 2 * T + hi],
+                scales=xs[(0, 4, 4, 0)[s] : P, s // 2 * T + lo : s // 2 * T + hi],
                 in_=xb[s][:, lo:hi, :].rearrange("p c t -> p (c t)"),
             )
 
-        def words(s, e, wide=False):
-            end = PASSES * T if wide else (s + 1) * T
-            gw[s, e] = keep.tile([P, C], U32, name="gw%d%d" % (s, e), align_bytes=64)
+        def words(s, experts, reach=1, tag=None):
+            n = len(experts) * C
+            lo = experts[0] * C // 16
+            codes = hold([P, n], U32, "gw%d%d" % (s, experts[0]), tag)
+            nc.vector.tensor_copy(codes[:], xw[:, s * T : (s + reach) * T].indirect(offs_t[:, lo : lo + n // 16]))
+            for i, e in enumerate(experts):
+                gw[s, e] = codes[:, i * C : (i + 1) * C]
+
+        def scales(h, experts, reach=1):
+            n = len(experts) * C
+            lo = experts[0] * C
             nc.vector.tensor_copy(
-                gw[s, e][:], xw[:, s * T : end].indirect(offs_t[:, e * C // 16 : (e + 1) * C // 16])
+                gs[h][:, lo : lo + n], xs[:, h * T : (h + reach) * T].indirect(offs_t[:, lo // 16 : (lo + n) // 16])
             )
 
-        def scales(h, experts, wide=False):
-            end = 2 * T if wide else (h + 1) * T
-            for e in experts:
-                nc.vector.tensor_copy(
-                    gs[h][:, e * C : (e + 1) * C],
-                    xs[:, h * T : end].indirect(offs_t[:, e * C // 16 : (e + 1) * C // 16]),
-                )
+        def unpack(h, experts, source=None):
             cols = slice(experts[0] * C, (experts[-1] + 1) * C)
+            packed = gs[h][:, cols] if source is None else source[:]
             for q in range(4):
                 nc.sync.dma_start(
                     out=gp[h][32 * q : 32 * q + 4, cols].bitcast(I32),
-                    in_=gs[h][32 * q + 4 : 32 * q + 8, cols].bitcast(I32),
+                    in_=packed[32 * q + 4 : 32 * q + 8, :].bitcast(I32),
                 )
+
+        def early_scales(e):
+            packed = hold([P, C], U8, "early%d" % e)
+            nc.vector.tensor_copy(packed[:], xs[:, T : 2 * T].indirect(offs_t[:, e * C // 16 : (e + 1) * C // 16]))
+            unpack(1, (e,), packed)
 
         acc = {}
 
@@ -138,122 +146,217 @@ def tile_moe_pln_mlp_relu2_kernel(
             e = b // 2
             if s == 0:
                 acc[b] = psum.tile([P, H], F32, name="bank")
-            cols = slice(b % 2 * P, (b % 2 + 1) * P)
-            plane = (gs if s % 2 == 0 else gp)[s // 2][:, b * P : (b + 1) * P]
-            w = (e * PASSES + s) * H
+            lo = b % 2 * P
             nc.tensor.matmul_mx(
                 out=acc[b][:],
-                lhsT=gw[s, e][:, cols].bitcast(FP8X4),
-                lhsT_scale=plane,
+                lhsT=gw[s, e][:, lo : lo + P].bitcast(FP8X4),
+                lhsT_scale=(gs[0], gp[0], gp[1], gs[1])[s][:, b * P : (b + 1) * P],
                 rhs=w1w[e][:, s * 2 * H : (s + 1) * 2 * H].bitcast(FP4X4),
-                rhs_scale=w1s[:, w : w + H],
+                rhs_scale=w1s[:, (e * PASSES + s) * H : (e * PASSES + s + 1) * H],
                 start=(s == 0),
                 stop=(s == PASSES - 1),
             )
 
-        def hidden(b):
-            cols = slice(b * P, (b + 1) * P)
-            r = work.tile([P, 4, P], F32, name="r", align_bytes=64)
+        rs, turned, hb, banks = {}, {}, {}, {}
+
+        def relu(b, engine):
+            rs[b] = work.tile([P, 4, P], F32, name="r", align_bytes=64)
             lanes = acc[b][:].rearrange("p (m t) -> p t m", t=4)
-            if b in VECTOR_RELU:
-                nc.vector.tensor_scalar_max(r[:], lanes, 0.0)
-            else:
-                nc.scalar.activation(r[:], lanes, RELU)
-            turned = aux.tile([P, 4, P], F32, name="aux")
-            for t in range(4):
-                nc.tensor.transpose(turned[:, t, :], r[:, t, :], ident[:])
-            hb = keep.tile([P, P, 4], BF16, name="hb%d" % b, align_bytes=64)
-            nc.scalar.activation(hb[:], turned[:].rearrange("p t n -> p n t"), SQUARE)
-            nc.vector.quantize_mx(
-                out=hw[:, cols].bitcast(FP8X4),
-                scales=hs[:, cols],
-                in_=hb[:].rearrange("p n t -> p (n t)"),
-            )
-
-        def second(e, j, bank):
-            w = e * N + j * P
-            nc.tensor.matmul_mx(
-                out=bank,
-                lhsT=w2w[:, 2 * w : 2 * (w + P)].bitcast(FP4X4),
-                lhsT_scale=w2s[:, w : w + P],
-                rhs=hw[:, e * C : (e + 1) * C].bitcast(FP8X4),
-                rhs_scale=hs[:, e * C : (e + 1) * C],
-                start=True,
-                stop=True,
-            )
-
-        def move(dst, src, engine):
             if engine == "v":
-                nc.vector.tensor_copy(dst, src)
+                nc.vector.tensor_scalar_max(rs[b][:], lanes, 0.0)
             else:
-                nc.scalar.copy(dst, src)
+                nc.scalar.activation(rs[b][:], lanes, RELU)
 
-        def load_tokens(s):
-            v = VECTOR_TOKENS[s]
-            cast(s, 0, v, "vector")
-            cast(s, v, T, "scalar")
-            if s == 0:
-                quantise(s, 0, half)
-                quantise(s, half, T)
+        def turn(b):
+            turned[b] = aux.tile([P, 4, P], F32, name="aux")
+            for t in range(4):
+                nc.tensor.transpose(turned[b][:, t, :], rs[b][:, t, :], ident[:])
+
+        def square(b):
+            hb[b] = hold([P, P, 4], BF16, "hb%d" % b)
+            nc.scalar.activation(hb[b][:], turned[b][:].rearrange("p t n -> p n t"), SQUARE)
+
+        def quantise_hidden(b):
+            nc.vector.quantize_mx(
+                out=hw[:, b * P : (b + 1) * P].bitcast(FP8X4),
+                scales=hs[:, b * P : (b + 1) * P],
+                in_=hb[b][:].rearrange("p n t -> p (n t)"),
+            )
+
+        def second(experts, j):
+            bank = banks[experts, j] = aux.tile([P, H], F32, name="aux")
+            for i, e in enumerate(experts):
+                w = e * N + j * P
+                nc.tensor.matmul_mx(
+                    out=bank[:, i * C : (i + 1) * C],
+                    lhsT=w2w[:, 2 * w : 2 * (w + P)].bitcast(FP4X4),
+                    lhsT_scale=w2s[:, w : w + P],
+                    rhs=hw[:, e * C : (e + 1) * C].bitcast(FP8X4),
+                    rhs_scale=hs[:, e * C : (e + 1) * C],
+                    start=True,
+                    stop=True,
+                )
+
+        def move(experts, j, engine):
+            bank = banks[experts, j]
+            lo = experts[0] * C
+            n = len(experts) * C
+            if engine == "v":
+                nc.vector.tensor_copy(y[j][:, lo : lo + n], bank[:, 0:n])
             else:
-                quantise(s, 0, T)
+                nc.scalar.copy(y[j][:, lo : lo + n], bank[:, 0:n])
 
-        load_tokens(0)
-        for e in range(E):
-            words(0, e)
-        load_tokens(1)
-        scales(0, (0, 1))
-        for e in (0, 1):
-            words(1, e)
-            for b in (2 * e, 2 * e + 1):
-                first(0, b)
-                first(1, b)
-        load_w1(2)
-        load_w1(3)
+        load_x(0, 0)
+        load_x(0, 1)
+        load_x(1)
+        cast(0, 256, 384, "v")
+        cast(0, 384, 512, "s")
+        cast(0, 0, 192, "v")
+        cast(0, 192, 256, "s")
+        load_w1_scales()
+        w2s = hold([P, E * N], U8, "w2s")
+        nc.vector.memset(w2s[:].bitcast(I32), 0)
         for q in range(4):
-            nc.sync.dma_start(
+            nc.gpsimd.dma_start(
                 out=w2s[32 * q : 32 * q + 4, :].bitcast(I32).rearrange("p (a b) -> p a b", b=N // 4),
                 in_=w2s_v[:, 0, 4 * q : 4 * q + 4, :].rearrange("e r b -> r e b"),
             )
+        load_x(2)
+        cast(2, 0, 512, "s")
+        cast(1, 0, 192, "v")
+        cast(1, 192, 512, "s")
+        load_x(3)
+        cast(3, 0, 512, "s")
+        quantise(0, 256, 512)
+        quantise(0, 0, 256)
+        quantise(1, 0, 512)
+        words(0, (2,), 1)
+        words(1, (0,), 1)
+        scales(0, (0,), 1)
+        scales(0, (1,), 1)
+        words(0, (1,), 1)
+        unpack(0, (0, 1))
+        quantise(2, 0, 512)
+        load_w1(0)
+        quantise(3, 0, 512)
+        scales(1, (0,))
+        words(0, (0,), 1)
+        scales(0, (2,), 2)
+        first(0, 1)
+        load_w1(2, "raw1")
+        scales(1, (1,))
+        scales(0, (3,), 2)
+        load_w1(1)
+        first(0, 2)
+        words(2, (1,), 1)
+        words(3, (0,))
+        words(1, (3,), 3)
+        first(0, 0)
+        first(1, 0)
+        words(0, (3,), 4)
+        first(0, 3)
+        unpack(1, (0,))
+        words(2, (0,), 1)
+        load_w1(3, "raw3")
+        first(2, 0)
+        scales(1, (2,))
+        first(1, 1)
+        first(3, 0)
+        first(2, 1)
+        first(0, 5)
+        words(1, (1,), 1)
+        unpack(1, (1,))
+        first(1, 3)
+        relu(0, "s")
+        nc.sync.dma_start(pos1_t[:], pos1)
+        nc.sync.dma_start(pos2_t[:], pos2)
+        words(3, (1,))
+        first(1, 2)
+        first(3, 1)
+        unpack(0, (2, 3))
+        scales(1, (3,))
+        words(1, (2,), 3)
+        first(2, 2)
+        first(0, 7)
+        relu(1, "s")
+        first(2, 3)
+        turn(1)
+        first(0, 6)
+        first(3, 2)
+        w2w = hold([P, E * 2 * N], U8, "w2w", "w2w")
         nc.sync.dma_start(
             out=w2w[:].bitcast(I32).rearrange("p (e b) -> p e b", e=E),
             in_=w2w_v[:, 0].rearrange("e p b -> p e b"),
         )
-        nc.sync.dma_start(pos1_t[:], pos1)
-        nc.sync.dma_start(pos2_t[:], pos2)
-        load_tokens(2)
-        load_tokens(3)
-        for e in (0, 1):
-            scales(1, (e,))
-            words(2, e, wide=True)
-            words(3, e)
-            for b in (2 * e, 2 * e + 1):
-                first(2, b)
-        scales(0, (2, 3), wide=True)
-        scales(1, (2, 3))
-        for e in (2, 3):
-            for s in range(1, PASSES):
-                words(s, e, wide=True)
-        g = late.tile([P, N // P, 2, T], F32, name="g", tag="late", align_bytes=64)
+        words(3, (3,), 1)
+        words(2, (2,), 2)
+        turn(0)
+        first(3, 3)
+        relu(2, "s")
+        square(0)
+        first(1, 6)
+        square(1)
+        turn(2)
+        quantise_hidden(0)
+        words(3, (2,), 1)
+        unpack(1, (2, 3))
+        first(1, 5)
+        first(0, 4)
+        relu(3, "s")
+        first(1, 4)
+        square(2)
+        turn(3)
+        square(3)
+        first(2, 4)
+        first(3, 4)
+        relu(4, "v")
+        quantise_hidden(2)
+        quantise_hidden(3)
+        turn(4)
+        first(2, 5)
+        first(3, 5)
+        words(2, (3,), 2)
+        quantise_hidden(1)
+        relu(5, "s")
+        first(2, 6)
+        g = hold([P, N // P, 2, T], F32, "g", "xs")
         for j in range(N // P):
             nc.sync.dma_start(out=g[:, j], in_=gate[:, j * P : (j + 1) * P, :].rearrange("g p t -> p g t"))
-        for b in range(4):
-            first(3, b)
-            hidden(b)
-        for b in range(4, 8):
-            for s in range(PASSES):
-                first(s, b)
-            hidden(b)
-        for j in range(N // P):
-            bank = aux.tile([P, H], F32, name="aux")
-            second(0, j, bank[:, 0:C])
-            second(1, j, bank[:, C : 2 * C])
-            move(y[j][:, 0 : 2 * C], bank[:], "vvv"[j])
-        for e in (2, 3):
-            for j in range(N // P):
-                bank = aux.tile([P, H], F32, name="aux")
-                second(e, j, bank[:, 0:C])
-                move(y[j][:, e * C : (e + 1) * C], bank[:, 0:C], ("svs", "vss")[e - 2][j])
+        square(4)
+        second((0, 1), 0)
+        move((0, 1), 0, "s")
+        first(3, 6)
+        first(1, 7)
+        turn(5)
+        relu(6, "s")
+        turn(6)
+        square(5)
+        quantise_hidden(5)
+        first(2, 7)
+        second((0, 1), 1)
+        square(6)
+        quantise_hidden(6)
+        quantise_hidden(4)
+        first(3, 7)
+        relu(7, "v")
+        turn(7)
+        second((2,), 0)
+        second((2,), 2)
+        square(7)
+        second((2,), 1)
+        move((2,), 1, "s")
+        quantise_hidden(7)
+        second((3,), 0)
+        second((3,), 2)
+        second((3,), 1)
+        move((0, 1), 1, "v")
+        move((3,), 1, "s")
+        move((2,), 0, "s")
+        move((2,), 2, "s")
+        second((0, 1), 2)
+        move((0, 1), 2, "s")
+        move((3,), 0, "v")
+        move((3,), 2, "s")
 
         for j in range(N // P):
             a = work.tile([P, T], F32, name="a")

@@ -31,8 +31,8 @@ def tile_moe_pln_mlp_relu2_kernel(
         lists = ctx.enter_context(tc.tile_pool(name="lists", bufs=1))
         keep = ctx.enter_context(tc.tile_pool(name="keep", bufs=1))
         work = ctx.enter_context(tc.tile_pool(name="work", bufs=4))
-        psum = ctx.enter_context(tc.psum_pool(name="psum", bufs=5))
-        aux = ctx.enter_context(tc.psum_pool(name="aux", bufs=3))
+        psum = ctx.enter_context(tc.psum_pool(name="psum", bufs=4))
+        aux = ctx.enter_context(tc.psum_pool(name="aux", bufs=4))
 
         def hold(shape, dtype, name, tag=None):
             return keep.tile(shape, dtype, name=name, tag=tag or name, align_bytes=64)
@@ -92,7 +92,20 @@ def tile_moe_pln_mlp_relu2_kernel(
         for h in range(2):
             nc.gpsimd.memset(gp[h][:].bitcast(I32), 0)
         make_identity(nc, ident[:])
-
+        load_x(0, 0)
+        load_x(0, 1)
+        load_w1_scales()
+        w2s = hold([P, E * N], U8, "w2s")
+        nc.vector.memset(w2s[:].bitcast(I32), 0)
+        for q in range(4):
+            nc.gpsimd.dma_start(
+                out=w2s[32 * q : 32 * q + 4, :].bitcast(I32).rearrange("p (a b) -> p a b", b=N // 4),
+                in_=w2s_v[:, 0, 4 * q : 4 * q + 4, :].rearrange("e r b -> r e b"),
+            )
+        load_x(1)
+        load_x(2)
+        load_x(3)
+        load_w1(0)
 
         def cast(s, lo, hi, engine):
             if hi > lo:
@@ -107,7 +120,7 @@ def tile_moe_pln_mlp_relu2_kernel(
         def quantise(s, lo, hi):
             nc.vector.quantize_mx(
                 out=xw[:, s * T + lo : s * T + hi].bitcast(FP8X4),
-                scales=xs[(0, 4, 4, 0)[s] : P, s // 2 * T + lo : s // 2 * T + hi],
+                scales=xs[4 * (s % 2) : P, s // 2 * T + lo : s // 2 * T + hi],
                 in_=xb[s][:, lo:hi, :].rearrange("p c t -> p (c t)"),
             )
 
@@ -126,19 +139,13 @@ def tile_moe_pln_mlp_relu2_kernel(
                 gs[h][:, lo : lo + n], xs[:, h * T : (h + reach) * T].indirect(offs_t[:, lo // 16 : (lo + n) // 16])
             )
 
-        def unpack(h, experts, source=None):
+        def unpack(h, experts):
             cols = slice(experts[0] * C, (experts[-1] + 1) * C)
-            packed = gs[h][:, cols] if source is None else source[:]
             for q in range(4):
                 nc.sync.dma_start(
                     out=gp[h][32 * q : 32 * q + 4, cols].bitcast(I32),
-                    in_=packed[32 * q + 4 : 32 * q + 8, :].bitcast(I32),
+                    in_=gs[h][32 * q + 4 : 32 * q + 8, cols].bitcast(I32),
                 )
-
-        def early_scales(e):
-            packed = hold([P, C], U8, "early%d" % e)
-            nc.vector.tensor_copy(packed[:], xs[:, T : 2 * T].indirect(offs_t[:, e * C // 16 : (e + 1) * C // 16]))
-            unpack(1, (e,), packed)
 
         acc = {}
 
@@ -150,41 +157,34 @@ def tile_moe_pln_mlp_relu2_kernel(
             nc.tensor.matmul_mx(
                 out=acc[b][:],
                 lhsT=gw[s, e][:, lo : lo + P].bitcast(FP8X4),
-                lhsT_scale=(gs[0], gp[0], gp[1], gs[1])[s][:, b * P : (b + 1) * P],
+                lhsT_scale=(gs, gp)[s % 2][s // 2][:, b * P : (b + 1) * P],
                 rhs=w1w[e][:, s * 2 * H : (s + 1) * 2 * H].bitcast(FP4X4),
                 rhs_scale=w1s[:, (e * PASSES + s) * H : (e * PASSES + s + 1) * H],
                 start=(s == 0),
                 stop=(s == PASSES - 1),
             )
 
-        rs, turned, hb, banks = {}, {}, {}, {}
-
-        def relu(b, engine):
-            rs[b] = work.tile([P, 4, P], F32, name="r", align_bytes=64)
+        def hidden(b, engine):
+            r = work.tile([P, 4, P], F32, name="r", align_bytes=64)
             lanes = acc[b][:].rearrange("p (m t) -> p t m", t=4)
             if engine == "v":
-                nc.vector.tensor_scalar_max(rs[b][:], lanes, 0.0)
+                nc.vector.tensor_scalar_max(r[:], lanes, 0.0)
             else:
-                nc.scalar.activation(rs[b][:], lanes, RELU)
-
-        def turn(b):
-            turned[b] = aux.tile([P, 4, P], F32, name="aux")
+                nc.scalar.activation(r[:], lanes, RELU)
+            turned = aux.tile([P, 4, P], F32, name="aux")
             for t in range(4):
-                nc.tensor.transpose(turned[b][:, t, :], rs[b][:, t, :], ident[:])
-
-        def square(b):
-            hb[b] = hold([P, P, 4], BF16, "hb%d" % b)
-            nc.scalar.activation(hb[b][:], turned[b][:].rearrange("p t n -> p n t"), SQUARE)
-
-        def quantise_hidden(b):
+                nc.tensor.transpose(turned[:, t, :], r[:, t, :], ident[:])
+            hb = hold([P, P, 4], BF16, "hb%d" % b)
+            nc.scalar.activation(hb[:], turned[:].rearrange("p t n -> p n t"), SQUARE)
             nc.vector.quantize_mx(
                 out=hw[:, b * P : (b + 1) * P].bitcast(FP8X4),
                 scales=hs[:, b * P : (b + 1) * P],
-                in_=hb[b][:].rearrange("p n t -> p (n t)"),
+                in_=hb[:].rearrange("p n t -> p (n t)"),
             )
 
-        def second(experts, j):
-            bank = banks[experts, j] = aux.tile([P, H], F32, name="aux")
+        def result(experts, j, engine):
+            n = len(experts) * C
+            bank = aux.tile([P, H], F32, name="aux")
             for i, e in enumerate(experts):
                 w = e * N + j * P
                 nc.tensor.matmul_mx(
@@ -196,173 +196,93 @@ def tile_moe_pln_mlp_relu2_kernel(
                     start=True,
                     stop=True,
                 )
-
-        def move(experts, j, engine):
-            bank = banks[experts, j]
             lo = experts[0] * C
-            n = len(experts) * C
             if engine == "v":
                 nc.vector.tensor_copy(y[j][:, lo : lo + n], bank[:, 0:n])
             else:
                 nc.scalar.copy(y[j][:, lo : lo + n], bank[:, 0:n])
 
-        load_x(0, 0)
-        load_x(0, 1)
-        load_x(1)
-        cast(0, 256, 384, "v")
-        cast(0, 384, 512, "s")
-        cast(0, 0, 192, "v")
-        cast(0, 192, 256, "s")
-        load_w1_scales()
-        w2s = hold([P, E * N], U8, "w2s")
-        nc.vector.memset(w2s[:].bitcast(I32), 0)
-        for q in range(4):
-            nc.gpsimd.dma_start(
-                out=w2s[32 * q : 32 * q + 4, :].bitcast(I32).rearrange("p (a b) -> p a b", b=N // 4),
-                in_=w2s_v[:, 0, 4 * q : 4 * q + 4, :].rearrange("e r b -> r e b"),
-            )
-        load_x(2)
-        cast(2, 0, 512, "s")
-        cast(1, 0, 192, "v")
-        cast(1, 192, 512, "s")
-        load_x(3)
-        cast(3, 0, 512, "s")
-        quantise(0, 256, 512)
-        quantise(0, 0, 256)
-        quantise(1, 0, 512)
-        words(0, (2,), 1)
-        words(1, (0,), 1)
-        scales(0, (0,), 1)
-        scales(0, (1,), 1)
-        words(0, (1,), 1)
+        for i, v in enumerate((128, 64)):
+            cast(0, i * half, i * half + v, "v")
+            cast(0, i * half + v, (i + 1) * half, "s")
+            quantise(0, i * half, (i + 1) * half)
+        for e in range(4):
+            words(0, (e,))
+        cast(1, 0, 128, "v")
+        cast(1, 128, T, "s")
+        quantise(1, 0, T)
+        load_w1(1, "raw1")
+        for e in (0, 1):
+            scales(0, (e,))
+            pass
         unpack(0, (0, 1))
-        quantise(2, 0, 512)
-        load_w1(0)
-        quantise(3, 0, 512)
-        scales(1, (0,))
-        words(0, (0,), 1)
-        scales(0, (2,), 2)
-        first(0, 1)
-        load_w1(2, "raw1")
-        scales(1, (1,))
-        scales(0, (3,), 2)
-        load_w1(1)
-        first(0, 2)
-        words(2, (1,), 1)
-        words(3, (0,))
-        words(1, (3,), 3)
-        first(0, 0)
-        first(1, 0)
-        words(0, (3,), 4)
-        first(0, 3)
-        unpack(1, (0,))
-        words(2, (0,), 1)
+        for e in (0, 1):
+            words(1, (e,))
+            for b in (2 * e, 2 * e + 1):
+                first(0, b)
+                first(1, b)
+        cast(2, 0, 0, "v")
+        cast(2, 0, T, "s")
+        quantise(2, 0, T)
+        for e in (0, 1):
+            words(2, (e,), 1)
+        load_w1(2, "raw2")
+        cast(3, 0, 192, "v")
+        cast(3, 192, T, "s")
+        quantise(3, 0, T)
+        for e in (0, 1):
+            scales(1, (e,))
+            unpack(1, (e,))
+            words(3, (e,))
+            for b in (2 * e, 2 * e + 1):
+                first(2, b)
         load_w1(3, "raw3")
-        first(2, 0)
-        scales(1, (2,))
-        first(1, 1)
-        first(3, 0)
-        first(2, 1)
-        first(0, 5)
-        words(1, (1,), 1)
-        unpack(1, (1,))
-        first(1, 3)
-        relu(0, "s")
-        nc.sync.dma_start(pos1_t[:], pos1)
-        nc.sync.dma_start(pos2_t[:], pos2)
-        words(3, (1,))
-        first(1, 2)
-        first(3, 1)
+        scales(0, (2, 3), 2)
         unpack(0, (2, 3))
+        scales(1, (2,))
         scales(1, (3,))
-        words(1, (2,), 3)
-        first(2, 2)
-        first(0, 7)
-        relu(1, "s")
-        first(2, 3)
-        turn(1)
-        first(0, 6)
-        first(3, 2)
-        w2w = hold([P, E * 2 * N], U8, "w2w", "w2w")
+        unpack(1, (2, 3))
+        for e in (2, 3):
+            for s in range(1, PASSES):
+                words(s, (e,), PASSES - s)
+        g = hold([P, N // P, 2, T], F32, "g", "xs")
+        for j in range(N // P):
+            nc.sync.dma_start(out=g[:, j], in_=gate[:, j * P : (j + 1) * P, :].rearrange("g p t -> p g t"))
+        for b in range(4):
+            first(3, b)
+            hidden(b, "ssssssss"[b])
+        w2w = hold([P, E * 2 * N], U8, "w2w", "xb3")
         nc.sync.dma_start(
             out=w2w[:].bitcast(I32).rearrange("p (e b) -> p e b", e=E),
             in_=w2w_v[:, 0].rearrange("e p b -> p e b"),
         )
-        words(3, (3,), 1)
-        words(2, (2,), 2)
-        turn(0)
-        first(3, 3)
-        relu(2, "s")
-        square(0)
-        first(1, 6)
-        square(1)
-        turn(2)
-        quantise_hidden(0)
-        words(3, (2,), 1)
-        unpack(1, (2, 3))
-        first(1, 5)
-        first(0, 4)
-        relu(3, "s")
-        first(1, 4)
-        square(2)
-        turn(3)
-        square(3)
-        first(2, 4)
-        first(3, 4)
-        relu(4, "v")
-        quantise_hidden(2)
-        quantise_hidden(3)
-        turn(4)
-        first(2, 5)
-        first(3, 5)
-        words(2, (3,), 2)
-        quantise_hidden(1)
-        relu(5, "s")
-        first(2, 6)
-        g = hold([P, N // P, 2, T], F32, "g", "xs")
+        nc.sync.dma_start(pos1_t[:], pos1)
+        nc.sync.dma_start(pos2_t[:], pos2)
+        for b in (4, 5):
+            for s in range(PASSES):
+                first(s, b)
+            hidden(b, "ssssssss"[b])
+        for b in (6, 7):
+            for s in range(PASSES):
+                first(s, b)
         for j in range(N // P):
-            nc.sync.dma_start(out=g[:, j], in_=gate[:, j * P : (j + 1) * P, :].rearrange("g p t -> p g t"))
-        square(4)
-        second((0, 1), 0)
-        move((0, 1), 0, "s")
-        first(3, 6)
-        first(1, 7)
-        turn(5)
-        relu(6, "s")
-        turn(6)
-        square(5)
-        quantise_hidden(5)
-        first(2, 7)
-        second((0, 1), 1)
-        square(6)
-        quantise_hidden(6)
-        quantise_hidden(4)
-        first(3, 7)
-        relu(7, "v")
-        turn(7)
-        second((2,), 0)
-        second((2,), 2)
-        square(7)
-        second((2,), 1)
-        move((2,), 1, "s")
-        quantise_hidden(7)
-        second((3,), 0)
-        second((3,), 2)
-        second((3,), 1)
-        move((0, 1), 1, "v")
-        move((3,), 1, "s")
-        move((2,), 0, "s")
-        move((2,), 2, "s")
-        second((0, 1), 2)
-        move((0, 1), 2, "s")
-        move((3,), 0, "v")
-        move((3,), 2, "s")
+            result((0, 1), j, "vvv"[j])
+        for b in (6, 7):
+            hidden(b, "ssssssss"[b])
 
         for j in range(N // P):
-            a = work.tile([P, T], F32, name="a")
-            b = work.tile([P, T], F32, name="b")
-            o = work.tile([P, T], F32, name="o")
-            nc.vector.tensor_tensor(a[:], y[j][:].indirect(pos1_t[:]), g[:, j, 0, :], MULT)
-            nc.vector.tensor_tensor(b[:], y[j][:].indirect(pos2_t[:]), g[:, j, 1, :], MULT)
-            nc.vector.tensor_tensor(o[:], a[:], b[:], ADD)
-            nc.sync.dma_start(out=out[j * P : (j + 1) * P, :], in_=o[:])
+            result((2,), j, "sss"[j])
+        for j in range(N // P):
+            result((3,), j, "vss"[j])
+
+        for j in range(N // P):
+            for lo, hi in ((0, T),) if j < 2 else ((0, T // 2), (T // 2, T)):
+                a = work.tile([P, T], F32, name="a")
+                b = work.tile([P, T], F32, name="b")
+                o = work.tile([P, T], F32, name="o")
+                n = slice(0, hi - lo)
+                cols = slice(lo // 16, hi // 16)
+                nc.vector.tensor_tensor(a[:, n], y[j][:].indirect(pos1_t[:, cols]), g[:, j, 0, lo:hi], MULT)
+                nc.vector.tensor_tensor(b[:, n], y[j][:].indirect(pos2_t[:, cols]), g[:, j, 1, lo:hi], MULT)
+                nc.vector.tensor_tensor(o[:, n], a[:, n], b[:, n], ADD)
+                nc.sync.dma_start(out=out[j * P : (j + 1) * P, lo:hi], in_=o[:, n])

from contextlib import ExitStack

import concourse.mybir as mybir
from concourse.masks import make_identity

K, T, E, C, H, N = 2048, 512, 4, 256, 512, 384
P = 128
PASSES = K // 512
SLOTS = E * C
FLOPS = 2 * SLOTS * (K * H + H * N)

F32 = mybir.dt.float32
BF16 = mybir.dt.bfloat16
I32 = mybir.dt.int32
U32 = mybir.dt.uint32
U16 = mybir.dt.uint16
U8 = mybir.dt.uint8
FP8X4 = mybir.dt.float8_e4m3fn_x4
FP4X4 = mybir.dt.float4_e2m1fn_x4
RELU = mybir.ActivationFunctionType.Relu
SQUARE = mybir.ActivationFunctionType.Square
MULT = mybir.AluOpType.mult
ADD = mybir.AluOpType.add


def tile_moe_pln_mlp_relu2_kernel(
    tc, xT, w1_words, w1_scales, w2_words, w2_scales, gate, offs, pos1, pos2, out
):
    nc = tc.nc
    with ExitStack() as ctx:
        lists = ctx.enter_context(tc.tile_pool(name="lists", bufs=1))
        keep = ctx.enter_context(tc.tile_pool(name="keep", bufs=1))
        work = ctx.enter_context(tc.tile_pool(name="work", bufs=4))
        psum = ctx.enter_context(tc.psum_pool(name="psum", bufs=4))
        aux = ctx.enter_context(tc.psum_pool(name="aux", bufs=4))

        def hold(shape, dtype, name, tag=None):
            return keep.tile(shape, dtype, name=name, tag=tag or name, align_bytes=64)

        offs_t = lists.tile([P, SLOTS // 16], U16, name="offs_t")
        pos1_t = lists.tile([P, T // 16], U16, name="pos1_t")
        pos2_t = lists.tile([P, T // 16], U16, name="pos2_t")

        xT_v = xT.rearrange("(s p j) t -> s p j t", p=P, j=4)
        w1w_v = w1_words.bitcast(I32)
        w1s_v = w1_scales.bitcast(I32)
        w2w_v = w2_words.bitcast(I32)
        w2s_v = w2_scales.bitcast(I32)

        half = T // 2
        raw = {}
        for i in range(2):
            raw[0, i] = hold([P, 4, half], F32, "raw0%d" % i)
        for s in range(1, PASSES):
            raw[s, 0] = hold([P, 4, T], F32, "raw%d" % s)
        xb = [hold([P, T, 4], BF16, "xb%d" % s) for s in range(PASSES)]
        xw = hold([P, PASSES * T], U32, "xw")
        xs = hold([P, 2 * T], U8, "xs")
        gw = {}
        gs = [hold([P, SLOTS], U8, "gs%d" % h) for h in range(2)]
        gp = [hold([P, SLOTS], U8, "gp%d" % h) for h in range(2)]
        w1s = hold([P, E * PASSES * H], U8, "w1s")
        w1w = {}
        hw = hold([P, SLOTS], U32, "hw")
        hs = hold([P, SLOTS], U8, "hs")
        y = [hold([P, SLOTS], F32, "y%d" % j) for j in range(N // P)]
        ident = hold([P, P], F32, "ident")

        def load_x(s, i=0):
            lo = i * half
            n = half if s == 0 else T
            nc.sync.dma_start(out=raw[s, i][:], in_=xT_v[s][:, :, lo : lo + n])

        def load_w1(e, tag=None):
            w1w[e] = hold([P, PASSES * 2 * H], U8, "w1w%d" % e, tag)
            nc.sync.dma_start(
                out=w1w[e][:].bitcast(I32).rearrange("p (s b) -> p s b", s=PASSES),
                in_=w1w_v[e].rearrange("s p b -> p s b"),
            )

        def load_w1_scales():
            for q in range(4):
                nc.gpsimd.dma_start(
                    out=w1s[32 * q : 32 * q + 4, :].bitcast(I32).rearrange("p (a b) -> p a b", b=H // 4),
                    in_=w1s_v[:, :, 4 * q : 4 * q + 4, :].rearrange("e s r b -> r (e s) b"),
                )

        nc.sync.dma_start(offs_t[:], offs)
        nc.vector.memset(w1s[:].bitcast(I32), 0)

        nc.gpsimd.memset(xs[:], 0)
        for h in range(2):
            nc.gpsimd.memset(gp[h][:].bitcast(I32), 0)
        make_identity(nc, ident[:])
        load_x(0, 0)
        load_x(0, 1)
        load_w1_scales()
        w2s = hold([P, E * N], U8, "w2s")
        nc.vector.memset(w2s[:].bitcast(I32), 0)
        for q in range(4):
            nc.gpsimd.dma_start(
                out=w2s[32 * q : 32 * q + 4, :].bitcast(I32).rearrange("p (a b) -> p a b", b=N // 4),
                in_=w2s_v[:, 0, 4 * q : 4 * q + 4, :].rearrange("e r b -> r e b"),
            )
        load_x(1)
        load_x(2)
        load_x(3)
        load_w1(0)

        def cast(s, lo, hi, engine):
            if hi > lo:
                i, base = (lo // half, lo // half * half) if s == 0 else (0, 0)
                dst = xb[s][:, lo:hi, :].rearrange("p (c i) t -> p c t i", i=4)
                src = raw[s, i][:, :, lo - base : hi - base].rearrange("p t (c i) -> p c t i", i=4)
                if engine == "v":
                    nc.vector.tensor_copy(dst, src)
                else:
                    nc.scalar.copy(dst, src)

        def quantise(s, lo, hi):
            nc.vector.quantize_mx(
                out=xw[:, s * T + lo : s * T + hi].bitcast(FP8X4),
                scales=xs[4 * (s % 2) : P, s // 2 * T + lo : s // 2 * T + hi],
                in_=xb[s][:, lo:hi, :].rearrange("p c t -> p (c t)"),
            )

        def words(s, experts, reach=1, tag=None):
            n = len(experts) * C
            lo = experts[0] * C // 16
            codes = hold([P, n], U32, "gw%d%d" % (s, experts[0]), tag)
            nc.vector.tensor_copy(codes[:], xw[:, s * T : (s + reach) * T].indirect(offs_t[:, lo : lo + n // 16]))
            for i, e in enumerate(experts):
                gw[s, e] = codes[:, i * C : (i + 1) * C]

        def scales(h, experts, reach=1):
            n = len(experts) * C
            lo = experts[0] * C
            nc.vector.tensor_copy(
                gs[h][:, lo : lo + n], xs[:, h * T : (h + reach) * T].indirect(offs_t[:, lo // 16 : (lo + n) // 16])
            )

        def unpack(h, experts):
            cols = slice(experts[0] * C, (experts[-1] + 1) * C)
            for q in range(4):
                nc.sync.dma_start(
                    out=gp[h][32 * q : 32 * q + 4, cols].bitcast(I32),
                    in_=gs[h][32 * q + 4 : 32 * q + 8, cols].bitcast(I32),
                )

        acc = {}

        def first(s, b):
            e = b // 2
            if s == 0:
                acc[b] = psum.tile([P, H], F32, name="bank")
            lo = b % 2 * P
            nc.tensor.matmul_mx(
                out=acc[b][:],
                lhsT=gw[s, e][:, lo : lo + P].bitcast(FP8X4),
                lhsT_scale=(gs, gp)[s % 2][s // 2][:, b * P : (b + 1) * P],
                rhs=w1w[e][:, s * 2 * H : (s + 1) * 2 * H].bitcast(FP4X4),
                rhs_scale=w1s[:, (e * PASSES + s) * H : (e * PASSES + s + 1) * H],
                start=(s == 0),
                stop=(s == PASSES - 1),
            )

        def hidden(b, engine):
            r = work.tile([P, 4, P], F32, name="r", align_bytes=64)
            lanes = acc[b][:].rearrange("p (m t) -> p t m", t=4)
            if engine == "v":
                nc.vector.tensor_scalar_max(r[:], lanes, 0.0)
            else:
                nc.scalar.activation(r[:], lanes, RELU)
            turned = aux.tile([P, 4, P], F32, name="aux")
            for t in range(4):
                nc.tensor.transpose(turned[:, t, :], r[:, t, :], ident[:])
            hb = hold([P, P, 4], BF16, "hb%d" % b)
            nc.scalar.activation(hb[:], turned[:].rearrange("p t n -> p n t"), SQUARE)
            nc.vector.quantize_mx(
                out=hw[:, b * P : (b + 1) * P].bitcast(FP8X4),
                scales=hs[:, b * P : (b + 1) * P],
                in_=hb[:].rearrange("p n t -> p (n t)"),
            )

        def result(experts, j, engine):
            n = len(experts) * C
            bank = aux.tile([P, H], F32, name="aux")
            for i, e in enumerate(experts):
                w = e * N + j * P
                nc.tensor.matmul_mx(
                    out=bank[:, i * C : (i + 1) * C],
                    lhsT=w2w[:, 2 * w : 2 * (w + P)].bitcast(FP4X4),
                    lhsT_scale=w2s[:, w : w + P],
                    rhs=hw[:, e * C : (e + 1) * C].bitcast(FP8X4),
                    rhs_scale=hs[:, e * C : (e + 1) * C],
                    start=True,
                    stop=True,
                )
            lo = experts[0] * C
            if engine == "v":
                nc.vector.tensor_copy(y[j][:, lo : lo + n], bank[:, 0:n])
            else:
                nc.scalar.copy(y[j][:, lo : lo + n], bank[:, 0:n])

        for i, v in enumerate((128, 64)):
            cast(0, i * half, i * half + v, "v")
            cast(0, i * half + v, (i + 1) * half, "s")
            quantise(0, i * half, (i + 1) * half)
        for e in range(4):
            words(0, (e,))
        cast(1, 0, 128, "v")
        cast(1, 128, T, "s")
        quantise(1, 0, T)
        load_w1(1, "raw1")
        for e in (0, 1):
            scales(0, (e,))
            pass
        unpack(0, (0, 1))
        for e in (0, 1):
            words(1, (e,))
            for b in (2 * e, 2 * e + 1):
                first(0, b)
                first(1, b)
        cast(2, 0, 0, "v")
        cast(2, 0, T, "s")
        quantise(2, 0, T)
        for e in (0, 1):
            words(2, (e,), 1)
        load_w1(2, "raw2")
        cast(3, 0, 192, "v")
        cast(3, 192, T, "s")
        quantise(3, 0, T)
        for e in (0, 1):
            scales(1, (e,))
            unpack(1, (e,))
            words(3, (e,))
            for b in (2 * e, 2 * e + 1):
                first(2, b)
        load_w1(3, "raw3")
        scales(0, (2, 3), 2)
        unpack(0, (2, 3))
        scales(1, (2,))
        scales(1, (3,))
        unpack(1, (2, 3))
        for e in (2, 3):
            for s in range(1, PASSES):
                words(s, (e,), PASSES - s)
        g = hold([P, N // P, 2, T], F32, "g", "xs")
        for j in range(N // P):
            nc.sync.dma_start(out=g[:, j], in_=gate[:, j * P : (j + 1) * P, :].rearrange("g p t -> p g t"))
        for b in range(4):
            first(3, b)
            hidden(b, "ssssssss"[b])
        w2w = hold([P, E * 2 * N], U8, "w2w", "xb3")
        nc.sync.dma_start(
            out=w2w[:].bitcast(I32).rearrange("p (e b) -> p e b", e=E),
            in_=w2w_v[:, 0].rearrange("e p b -> p e b"),
        )
        nc.sync.dma_start(pos1_t[:], pos1)
        nc.sync.dma_start(pos2_t[:], pos2)
        for b in (4, 5):
            for s in range(PASSES):
                first(s, b)
            hidden(b, "ssssssss"[b])
        for b in (6, 7):
            for s in range(PASSES):
                first(s, b)
        for j in range(N // P):
            result((0, 1), j, "vvv"[j])
        for b in (6, 7):
            hidden(b, "ssssssss"[b])

        for j in range(N // P):
            result((2,), j, "sss"[j])
        for j in range(N // P):
            result((3,), j, "vss"[j])

        for j in range(N // P):
            for lo, hi in ((0, T),) if j < 2 else ((0, T // 2), (T // 2, T)):
                a = work.tile([P, T], F32, name="a")
                b = work.tile([P, T], F32, name="b")
                o = work.tile([P, T], F32, name="o")
                n = slice(0, hi - lo)
                cols = slice(lo // 16, hi // 16)
                nc.vector.tensor_tensor(a[:, n], y[j][:].indirect(pos1_t[:, cols]), g[:, j, 0, lo:hi], MULT)
                nc.vector.tensor_tensor(b[:, n], y[j][:].indirect(pos2_t[:, cols]), g[:, j, 1, lo:hi], MULT)
                nc.vector.tensor_tensor(o[:, n], a[:, n], b[:, n], ADD)
                nc.sync.dma_start(out=out[j * P : (j + 1) * P, lo:hi], in_=o[:, n])
